import numpy as np
import ml_dtypes


def mxq(x, axis, fmt="e4m3"):
    dtype, down = {"e4m3": (ml_dtypes.float8_e4m3fn, 7), "e5m2": (ml_dtypes.float8_e5m2, 14)}[fmt]
    v = np.moveaxis(np.asarray(x, np.float32).astype(ml_dtypes.bfloat16).astype(np.float64), axis, -1)
    blocks = v.reshape(v.shape[:-1] + (-1, 32))
    amax = np.abs(blocks).max(-1, keepdims=True)
    byte = np.maximum(np.where(amax > 0, np.frexp(amax)[1] - 1 + 127, 0) - down, 1)
    scale = np.exp2(byte - 127.0)
    codes = (blocks / scale).astype(np.float32).astype(dtype).astype(np.float64)
    return np.moveaxis((codes * scale).reshape(v.shape), -1, axis)


WIDE = False


def mx_kscale(k):
    if not WIDE:
        return np.ones(k)
    levels = np.array([10, -10, 5, -5, 0])
    if k % 512:
        return np.exp2(np.random.permutation(np.resize(levels, k // 32))).repeat(32)
    a = np.empty((k // 512, 16))
    for p in range(k // 512):
        a[p, :8] = np.random.permutation(np.resize(levels, 8))
        for g in range(8):
            far = levels[np.abs(levels - a[p, g]) >= 10]
            a[p, g + 8] = far[np.random.randint(len(far))]
    return np.exp2(a.ravel()).repeat(32)


def f64(x):
    return np.asarray(x).astype(np.float64)


def striped(idx):
    return np.tile(idx.reshape(-1, 16).T, (8, 1)).astype(np.uint16)


def unstriped(offs):
    return offs[:16].T.reshape(-1).astype(np.int64)


def pack_weight(w):
    k, n = w.shape
    w = f64(np.asarray(w, np.float32).astype(ml_dtypes.bfloat16)).reshape(k // 32, 32, n)
    amax = np.abs(w).max(1)
    byte = np.clip(np.where(amax > 0, np.frexp(amax)[1] - 1 + 127 - 7, 1), 1, 254)
    scaled = (w * np.exp2(127.0 - byte)[:, None, :]).reshape(k, n).astype(np.float32)
    words = np.ascontiguousarray(scaled.reshape(k // 512, 128, 4, n).transpose(0, 1, 3, 2)).astype(ml_dtypes.float8_e4m3fn).view(np.uint8)
    return words, np.ascontiguousarray(byte.astype(np.uint8).reshape(k // 512, 16, n))


def unpack_weight(words, scales):
    g, p, n, _ = words.shape
    vals = np.ascontiguousarray(words).view(ml_dtypes.float8_e4m3fn).astype(np.float64) * np.repeat(np.exp2(scales.astype(np.float64) - 127.0), 8, axis=1)[..., None]
    return vals.transpose(0, 1, 3, 2).reshape(g * 512, n)


def sigmoid(v):
    return 1.0 / (1.0 + np.exp(-np.maximum(v, -700.0)))


K, T, S, D, N, H = 1024, 4096, 1024, 4, 128, 512


def setup_inputs():
    n = np.random.standard_normal
    s = mx_kscale(K)[:, None]
    u = mx_kscale(H)
    packed_xT = pack_weight(n((K, T)) * s)
    return {
        "x_words": packed_xT[0],
        "x_scales": packed_xT[1],
        "w1": (n((K, H)) / np.sqrt(K) / s).astype(np.float32),
        "xn": (np.random.uniform(0.3, 1.5, (H, S))).astype(np.float32),
        "unit": (np.random.uniform(0.6, 1.4, (H, 1)) * u[:, None]).astype(np.float32),
        "w2": (n((H, N)) / np.sqrt(H) / u[:, None]).astype(np.float32),
        "offs": striped(np.random.permutation(T)[:S]),
        "pt": striped(np.random.permutation(S)),
    }


def reference(x_words, x_scales, w1, xn, unit, w2, offs, pt):
    xq = unpack_weight(x_words, x_scales)[:, unstriped(offs)]
    y = mxq(f64(w1), 0, "e4m3").T @ xq
    mag = np.abs(y)
    sal = mag * f64(xn)
    best = sal.reshape(len(sal), -1, D).max(axis=2)
    keepw = sigmoid(5.0 * (sal - (0.6 * np.repeat(best, D, axis=1))))
    drop = (-1.0 * keepw + 1.0) * y
    dropp = drop[:, unstriped(pt)]
    comp = keepw * y + 0.5 * dropp
    hid = f64(unit) * comp
    return mxq(f64(w2), 0, "e4m3").T @ mxq(hid, 0, "e4m3")

@@ -1,0 +1,212 @@
+from contextlib import ExitStack
+
+import concourse.mybir as mybir
+
+K, T, S, D, N, H = 1024, 4096, 1024, 4, 128, 512
+FLOPS = 2 * K * H * S + 2 * H * N * S
+
+F32 = mybir.dt.float32
+BF16 = mybir.dt.bfloat16
+I32 = mybir.dt.int32
+U32 = mybir.dt.uint32
+U16 = mybir.dt.uint16
+U8 = mybir.dt.uint8
+FP8X4 = mybir.dt.float8_e4m3fn_x4
+ALU = mybir.AluOpType
+ACT = mybir.ActivationFunctionType
+
+P = 128
+PACK = 4
+PASSES = K // (P * PACK)
+HALF = 512
+HALVES = S // HALF
+CHUNK = 256
+STRIPE = 16
+
+
+def tile_picked_ylisax_comp_p_kernel(
+    tc, x_words, x_scales, w1, xn, unit, w2, offs, pt, out
+):
+    nc = tc.nc
+    with ExitStack() as ctx:
+        keep = ctx.enter_context(tc.tile_pool(name="keep", bufs=1))
+        ring = ctx.enter_context(tc.tile_pool(name="ring", bufs=3))
+        psum = ctx.enter_context(tc.psum_pool(name="psum", bufs=8))
+
+        offs_sb = keep.tile([P, S // STRIPE], U16, name="offs_sb")
+        pt_sb = keep.tile([P, S // STRIPE], U16, name="pt_sb")
+        nc.sync.dma_start(offs_sb[:], offs)
+        nc.sync.dma_start(pt_sb[:], pt)
+
+        x_scale_win = keep.tile([P, T], U8, name="x_scale_win", align_bytes=64)
+        nc.vector.memset(x_scale_win[:].bitcast(I32), 0)
+        for q in range(4):
+            nc.scalar.dma_start(
+                x_scale_win[32 * q : 32 * q + 4 * PASSES, :].bitcast(I32),
+                x_scales[:, 4 * q : 4 * q + 4, :].bitcast(I32),
+            )
+
+        w1_rows = w1.rearrange("(o p j) c -> o p j c", p=P, j=PACK)
+        w1_raw0 = keep.tile([P, PACK * H], F32, name="w1_raw0", tag="stage")
+        nc.sync.dma_start(w1_raw0[:].rearrange("p (j c) -> p j c", j=PACK), w1_rows[0])
+
+        x_win = []
+        for o in range(PASSES):
+            win = keep.tile([P, T], U32, name=f"x_win{o}", align_bytes=64)
+            nc.sync.dma_start(win[:].bitcast(I32), x_words[o].rearrange("p n t -> p (n t)").bitcast(I32))
+            x_win.append(win)
+
+        w1_raw1 = []
+        for a in range(2):
+            raw = keep.tile([P, PACK, H // 2], F32, name=f"w1_raw1_{a}")
+            nc.sync.dma_start(raw[:], w1_rows[1][:, :, a * (H // 2) : (a + 1) * (H // 2)])
+            w1_raw1.append(raw)
+
+        w1_bf = [keep.tile([P, PACK * H], BF16, name=f"w1_bf{o}", align_bytes=64) for o in range(PASSES)]
+        w1_codes = [keep.tile([P, H], U32, name=f"w1_codes{o}", align_bytes=64) for o in range(PASSES)]
+        w1_scales = [keep.tile([P, H], U8, name=f"w1_scales{o}", align_bytes=64) for o in range(PASSES)]
+
+        def dealt(o):
+            return w1_bf[o][:].rearrange("p (t m j) -> p m j t", t=PACK, j=PACK)
+
+        nc.scalar.activation(dealt(0), w1_raw0[:].rearrange("p (j m t) -> p m j t", j=PACK, t=PACK), ACT.Copy)
+        nc.vector.quantize_mx(out=w1_codes[0][:].bitcast(FP8X4), scales=w1_scales[0][:], in_=w1_bf[0][:])
+
+        late = keep.tile([P, PACK * S + PACK * N + PACK], F32, name="late", tag="stage")
+        xn_rows = xn.rearrange("(p t) j -> p t j", t=PACK)
+        unit_sb = late[:, PACK * S + PACK * N :]
+        w2_raw = late[:, PACK * S : PACK * S + PACK * N]
+        nc.sync.dma_start(late[:, 0:S], xn_rows[:, 0, :])
+        nc.sync.dma_start(unit_sb, unit.rearrange("(p t) o -> p (t o)", t=PACK))
+        for t in range(1, PACK):
+            nc.sync.dma_start(late[:, t * S : (t + 1) * S], xn_rows[:, t, :])
+        nc.sync.dma_start(w2_raw, w2.rearrange("(p j) n -> p (j n)", j=PACK))
+
+        def entries(lst, first, count):
+            return lst[:, first // STRIPE : (first + count) // STRIPE]
+
+        xg_scales = []
+        for h in range(HALVES):
+            g = keep.tile([P, HALF], U8, name=f"xg_scales{h}", align_bytes=64)
+            nc.vector.tensor_copy(g[:], x_scale_win[:].indirect(entries(offs_sb, h * HALF, HALF)))
+            xg_scales.append(g)
+        xg_words = {}
+        for o in range(PASSES):
+            for h in range(HALVES):
+                g = keep.tile([P, HALF], U32, name=f"xg_words{o}_{h}", align_bytes=64)
+                nc.vector.tensor_copy(g[:], x_win[o][:].indirect(entries(offs_sb, h * HALF, HALF)))
+                xg_words[o, h] = g
+
+        half_m = P // 2
+        nc.scalar.copy(dealt(1)[:, 0:half_m], w1_raw1[0][:].rearrange("p j (m t) -> p m j t", t=PACK))
+        nc.vector.tensor_copy(dealt(1)[:, half_m:P], w1_raw1[1][:].rearrange("p j (m t) -> p m j t", t=PACK))
+        for t in range(PACK):
+            nc.vector.quantize_mx(
+                out=w1_codes[1][:, t * P : (t + 1) * P].bitcast(FP8X4),
+                scales=w1_scales[1][:, t * P : (t + 1) * P],
+                in_=w1_bf[1][:, t * P * PACK : (t + 1) * P * PACK],
+            )
+
+        y = {}
+        for t in range(PACK):
+            for h in range(HALVES):
+                y[t, h] = psum.tile([P, HALF], F32, name=f"y{t}_{h}", tag="bank")
+        for o in range(PASSES):
+            for t in range(PACK):
+                for h in range(HALVES):
+                    nc.tensor.matmul_mx(
+                        out=y[t, h][:],
+                        lhsT=w1_codes[o][:, t * P : (t + 1) * P].bitcast(FP8X4),
+                        lhsT_scale=w1_scales[o][:, t * P : (t + 1) * P],
+                        rhs=xg_words[o, h][:].bitcast(FP8X4),
+                        rhs_scale=xg_scales[h][4 * o : P, :],
+                        start=(o == 0),
+                        stop=(o == PASSES - 1),
+                    )
+
+        drop = [keep.tile([P, S], F32, name=f"drop{t}") for t in range(PACK)]
+        kept = [keep.tile([P, PACK, HALF], F32, name=f"kept{h}") for h in range(HALVES)]
+        fetched = [keep.tile([P, PACK, CHUNK], F32, name=f"fetched{c}") for c in range(S // CHUNK)]
+        gate = {}
+
+        def salience(t, h):
+            mag = ring.tile([P, HALF], F32, name="mag")
+            nc.scalar.activation(mag[:], y[t, h][:], ACT.Abs)
+            sal = ring.tile([P, HALF // D, D], F32, name="sal")
+            first = t * S + h * HALF
+            nc.vector.tensor_tensor(
+                sal[:].rearrange("p v d -> p (v d)"), mag[:], late[:, first : first + HALF], ALU.mult
+            )
+            pair = ring.tile([P, HALF // D, 2], F32, name="pair")
+            nc.vector.tensor_tensor(pair[:], sal[:, :, 0:2], sal[:, :, 2:4], ALU.max)
+            best = ring.tile([P, HALF // D, 1], F32, name="best")
+            nc.vector.tensor_tensor(best[:], pair[:, :, 0:1], pair[:, :, 1:2], ALU.max)
+            arg = ring.tile([P, HALF // D, D], F32, name="arg")
+            nc.vector.scalar_tensor_tensor(
+                arg[:], best[:].to_broadcast([P, HALF // D, D]), -0.6, sal[:], ALU.mult, ALU.add
+            )
+            lose = ring.tile([P, HALF], F32, name="lose")
+            nc.scalar.activation(lose[:], arg[:].rearrange("p v d -> p (v d)"), ACT.Sigmoid, scale=-5.0)
+            gate[t, h] = lose
+
+        def dropped(t, h):
+            cols = slice(h * HALF, (h + 1) * HALF)
+            u = unit_sb[:, t : t + 1]
+            nc.vector.scalar_tensor_tensor(drop[t][:, cols], y[t, h][:], u, gate[t, h][:], ALU.mult, ALU.mult)
+
+        def remains(t, h):
+            cols = slice(h * HALF, (h + 1) * HALF)
+            u = unit_sb[:, t : t + 1]
+            nc.vector.scalar_tensor_tensor(kept[h][:, t, :], y[t, h][:], u, drop[t][:, cols], ALU.mult, ALU.subtract)
+
+        def fetch(t):
+            for c in range(S // CHUNK):
+                nc.scalar.activation(
+                    fetched[c][:, t, :], drop[t][:].indirect(entries(pt_sb, c * CHUNK, CHUNK)), ACT.Copy, scale=0.5
+                )
+
+        units = [(t, h) for t in range(PACK) for h in range(HALVES)]
+        salience(*units[0])
+        for n, (t, h) in enumerate(units):
+            if n + 1 < len(units):
+                salience(*units[n + 1])
+            dropped(t, h)
+            if h == HALVES - 1:
+                fetch(t)
+                for g in range(HALVES):
+                    remains(t, g)
+
+        w2_bf = keep.tile([P, N * PACK], BF16, name="w2_bf", align_bytes=64)
+        w2_codes = keep.tile([P, N], U32, name="w2_codes", align_bytes=64)
+        w2_scales = keep.tile([P, N], U8, name="w2_scales", align_bytes=64)
+        nc.scalar.copy(
+            w2_bf[:].rearrange("p (c i j) -> p c j i", i=4, j=PACK),
+            w2_raw.rearrange("p (j c i) -> p c j i", j=PACK, i=4),
+        )
+        nc.vector.quantize_mx(out=w2_codes[:].bitcast(FP8X4), scales=w2_scales[:], in_=w2_bf[:])
+
+        for c in range(S // CHUNK):
+            h, first = divmod(c * CHUNK, HALF)
+            hid = ring.tile([P, CHUNK * PACK], BF16, name="hid", align_bytes=64)
+            nc.vector.tensor_tensor(
+                hid[:].rearrange("p (c i t) -> p c t i", i=4, t=PACK),
+                kept[h][:, :, first : first + CHUNK].rearrange("p t (c i) -> p c t i", i=4),
+                fetched[c][:].rearrange("p t (c i) -> p c t i", i=4),
+                ALU.add,
+            )
+            hid_codes = ring.tile([P, CHUNK], U32, name="hid_codes", align_bytes=64)
+            hid_scales = ring.tile([P, CHUNK], U8, name="hid_scales", align_bytes=64)
+            nc.vector.quantize_mx(out=hid_codes[:].bitcast(FP8X4), scales=hid_scales[:], in_=hid[:])
+            acc = psum.tile([P, CHUNK], F32, name="acc", tag="bank")
+            nc.tensor.matmul_mx(
+                out=acc[:],
+                lhsT=w2_codes[:].bitcast(FP8X4),
+                lhsT_scale=w2_scales[:],
+                rhs=hid_codes[:].bitcast(FP8X4),
+                rhs_scale=hid_scales[:],
+                start=True,
+                stop=True,
+            )
+            result = ring.tile([P, CHUNK], F32, name="result")
+            nc.scalar.copy(result[:], acc[:])
+            nc.sync.dma_start(out[:, c * CHUNK : (c + 1) * CHUNK], result[:])

@@ -36,76 +36,62 @@ def tile_picked_ylisax_comp_p_kernel(
         offs_sb = keep.tile([P, S // STRIPE], U16, name="offs_sb")
         pt_sb = keep.tile([P, S // STRIPE], U16, name="pt_sb")
         nc.sync.dma_start(offs_sb[:], offs)
-        nc.sync.dma_start(pt_sb[:], pt)
 
         x_scale_win = keep.tile([P, T], U8, name="x_scale_win", align_bytes=64)
         nc.vector.memset(x_scale_win[:].bitcast(I32), 0)
         for q in range(4):
-            nc.scalar.dma_start(
+            nc.gpsimd.dma_start(
                 x_scale_win[32 * q : 32 * q + 4 * PASSES, :].bitcast(I32),
                 x_scales[:, 4 * q : 4 * q + 4, :].bitcast(I32),
             )
 
-        w1_rows = w1.rearrange("(o p j) c -> o p j c", p=P, j=PACK)
-        w1_raw0 = keep.tile([P, PACK * H], F32, name="w1_raw0", tag="stage")
-        nc.sync.dma_start(w1_raw0[:].rearrange("p (j c) -> p j c", j=PACK), w1_rows[0])
-
-        x_win = []
+        w1_rows = w1.rearrange("(o p j) c -> o p (j c)", p=P, j=PACK)
+        w1_raw, x_win = [], []
+        for o in range(PASSES):
+            raw = keep.tile([P, PACK * H], F32, name=f"w1_raw{o}", tag=f"stage{o}")
+            nc.sync.dma_start(raw[:], w1_rows[o])
+            w1_raw.append(raw)
         for o in range(PASSES):
             win = keep.tile([P, T], U32, name=f"x_win{o}", align_bytes=64)
             nc.sync.dma_start(win[:].bitcast(I32), x_words[o].rearrange("p n t -> p (n t)").bitcast(I32))
             x_win.append(win)
-
-        w1_raw1 = []
-        for a in range(2):
-            raw = keep.tile([P, PACK, H // 2], F32, name=f"w1_raw1_{a}")
-            nc.sync.dma_start(raw[:], w1_rows[1][:, :, a * (H // 2) : (a + 1) * (H // 2)])
-            w1_raw1.append(raw)
-
-        w1_bf = [keep.tile([P, PACK * H], BF16, name=f"w1_bf{o}", align_bytes=64) for o in range(PASSES)]
-        w1_codes = [keep.tile([P, H], U32, name=f"w1_codes{o}", align_bytes=64) for o in range(PASSES)]
-        w1_scales = [keep.tile([P, H], U8, name=f"w1_scales{o}", align_bytes=64) for o in range(PASSES)]
-
-        def dealt(o):
-            return w1_bf[o][:].rearrange("p (t m j) -> p m j t", t=PACK, j=PACK)
-
-        nc.scalar.activation(dealt(0), w1_raw0[:].rearrange("p (j m t) -> p m j t", j=PACK, t=PACK), ACT.Copy)
-        nc.vector.quantize_mx(out=w1_codes[0][:].bitcast(FP8X4), scales=w1_scales[0][:], in_=w1_bf[0][:])
-
-        late = keep.tile([P, PACK * S + PACK * N + PACK], F32, name="late", tag="stage")
-        xn_rows = xn.rearrange("(p t) j -> p t j", t=PACK)
-        unit_sb = late[:, PACK * S + PACK * N :]
-        w2_raw = late[:, PACK * S : PACK * S + PACK * N]
-        nc.sync.dma_start(late[:, 0:S], xn_rows[:, 0, :])
-        nc.sync.dma_start(unit_sb, unit.rearrange("(p t) o -> p (t o)", t=PACK))
-        for t in range(1, PACK):
-            nc.sync.dma_start(late[:, t * S : (t + 1) * S], xn_rows[:, t, :])
-        nc.sync.dma_start(w2_raw, w2.rearrange("(p j) n -> p (j n)", j=PACK))
+        nc.sync.dma_start(pt_sb[:], pt)
 
         def entries(lst, first, count):
             return lst[:, first // STRIPE : (first + count) // STRIPE]
 
-        xg_scales = []
-        for h in range(HALVES):
-            g = keep.tile([P, HALF], U8, name=f"xg_scales{h}", align_bytes=64)
-            nc.vector.tensor_copy(g[:], x_scale_win[:].indirect(entries(offs_sb, h * HALF, HALF)))
-            xg_scales.append(g)
-        xg_words = {}
+        w1_codes, w1_scales, xg_scales, xg_words = [], [], [], {}
         for o in range(PASSES):
+            grouped = keep.tile([P, PACK * H], BF16, name=f"w1_bf{o}", align_bytes=64)
+            codes = keep.tile([P, H], U32, name=f"w1_codes{o}", align_bytes=64)
+            scales = keep.tile([P, H], U8, name=f"w1_scales{o}", align_bytes=64)
+            nc.scalar.activation(
+                grouped[:].rearrange("p (t m j) -> p t m j", t=PACK, j=PACK),
+                w1_raw[o][:].rearrange("p (j m t) -> p t m j", j=PACK, t=PACK),
+                ACT.Copy,
+            )
+            if o == 0:
+                for h in range(HALVES):
+                    g = keep.tile([P, HALF], U8, name=f"xg_scales{h}", align_bytes=64)
+                    nc.vector.tensor_copy(g[:], x_scale_win[:].indirect(entries(offs_sb, h * HALF, HALF)))
+                    xg_scales.append(g)
+            nc.vector.quantize_mx(out=codes[:].bitcast(FP8X4), scales=scales[:], in_=grouped[:])
+            w1_codes.append(codes)
+            w1_scales.append(scales)
             for h in range(HALVES):
                 g = keep.tile([P, HALF], U32, name=f"xg_words{o}_{h}", align_bytes=64)
                 nc.vector.tensor_copy(g[:], x_win[o][:].indirect(entries(offs_sb, h * HALF, HALF)))
                 xg_words[o, h] = g
 
-        half_m = P // 2
-        nc.scalar.copy(dealt(1)[:, 0:half_m], w1_raw1[0][:].rearrange("p j (m t) -> p m j t", t=PACK))
-        nc.vector.tensor_copy(dealt(1)[:, half_m:P], w1_raw1[1][:].rearrange("p j (m t) -> p m j t", t=PACK))
+        late = keep.tile([P, PACK * S + PACK * N + PACK], F32, name="late", tag="stage0")
+        xn_rows = xn.rearrange("(p t) j -> p t j", t=PACK)
+        unit_sb = late[:, PACK * S + PACK * N :]
+        w2_raw = late[:, PACK * S : PACK * S + PACK * N]
         for t in range(PACK):
-            nc.vector.quantize_mx(
-                out=w1_codes[1][:, t * P : (t + 1) * P].bitcast(FP8X4),
-                scales=w1_scales[1][:, t * P : (t + 1) * P],
-                in_=w1_bf[1][:, t * P * PACK : (t + 1) * P * PACK],
-            )
+            nc.sync.dma_start(late[:, t * S : (t + 1) * S], xn_rows[:, t, :])
+            if t == 1:
+                nc.sync.dma_start(unit_sb, unit.rearrange("(p t) o -> p (t o)", t=PACK))
+        nc.sync.dma_start(w2_raw, w2.rearrange("(p j) n -> p (j n)", j=PACK))
 
         y = {}
         for t in range(PACK):
@@ -127,76 +113,109 @@ def tile_picked_ylisax_comp_p_kernel(
         drop = [keep.tile([P, S], F32, name=f"drop{t}") for t in range(PACK)]
         kept = [keep.tile([P, PACK, HALF], F32, name=f"kept{h}") for h in range(HALVES)]
         fetched = [keep.tile([P, PACK, CHUNK], F32, name=f"fetched{c}") for c in range(S // CHUNK)]
-        gate = {}
+        G = S // D
+        mag = [keep.tile([P, S], F32, name=f"mag{t}") for t in range(PACK)]
+        sal = [keep.tile([P, S], F32, name=f"sal{t}") for t in range(PACK)]
+        pair = [keep.tile([P, 2 * G], F32, name=f"pair{t}") for t in range(PACK)]
+        best = [keep.tile([P, G], F32, name=f"best{t}") for t in range(PACK)]
+        arg = [keep.tile([P, S], F32, name=f"arg{t}") for t in range(PACK)]
+        lose = [keep.tile([P, S], F32, name=f"lose{t}") for t in range(PACK)]
 
-        def salience(t, h):
-            mag = ring.tile([P, HALF], F32, name="mag")
-            nc.scalar.activation(mag[:], y[t, h][:], ACT.Abs)
-            sal = ring.tile([P, HALF // D, D], F32, name="sal")
-            first = t * S + h * HALF
+        def half(h):
+            return slice(h * HALF, (h + 1) * HALF)
+
+        def magnitude(t):
+            for h in range(HALVES):
+                nc.scalar.activation(mag[t][:, half(h)], y[t, h][:], ACT.Abs)
+
+        def salience(t, cols):
+            nc.vector.tensor_tensor(sal[t][:, cols], mag[t][:, cols], late[:, t * S : (t + 1) * S][:, cols], ALU.mult)
+
+        def max_pairs(t):
+            groups = sal[t][:].rearrange("p (v d) -> p v d", d=D)
             nc.vector.tensor_tensor(
-                sal[:].rearrange("p v d -> p (v d)"), mag[:], late[:, first : first + HALF], ALU.mult
+                pair[t][:].rearrange("p (v e) -> p v e", e=2), groups[:, :, 0:2], groups[:, :, 2:4], ALU.max
             )
-            pair = ring.tile([P, HALF // D, 2], F32, name="pair")
-            nc.vector.tensor_tensor(pair[:], sal[:, :, 0:2], sal[:, :, 2:4], ALU.max)
-            best = ring.tile([P, HALF // D, 1], F32, name="best")
-            nc.vector.tensor_tensor(best[:], pair[:, :, 0:1], pair[:, :, 1:2], ALU.max)
-            arg = ring.tile([P, HALF // D, D], F32, name="arg")
+
+        def max_groups(t):
+            nc.vector.tensor_tensor(best[t][:], pair[t][:, 0::2], pair[t][:, 1::2], ALU.max)
+
+        def gate(t):
             nc.vector.scalar_tensor_tensor(
-                arg[:], best[:].to_broadcast([P, HALF // D, D]), -0.6, sal[:], ALU.mult, ALU.add
+                arg[t][:].rearrange("p (v d) -> p v d", d=D),
+                best[t][:].unsqueeze(2).to_broadcast([P, G, D]),
+                -0.6,
+                sal[t][:].rearrange("p (v d) -> p v d", d=D),
+                ALU.mult,
+                ALU.add,
             )
-            lose = ring.tile([P, HALF], F32, name="lose")
-            nc.scalar.activation(lose[:], arg[:].rearrange("p v d -> p (v d)"), ACT.Sigmoid, scale=-5.0)
-            gate[t, h] = lose
+            for h in range(HALVES):
+                nc.scalar.activation(lose[t][:, half(h)], arg[t][:, half(h)], ACT.Sigmoid, scale=-5.0)
 
         def dropped(t, h):
-            cols = slice(h * HALF, (h + 1) * HALF)
-            u = unit_sb[:, t : t + 1]
-            nc.vector.scalar_tensor_tensor(drop[t][:, cols], y[t, h][:], u, gate[t, h][:], ALU.mult, ALU.mult)
+            nc.vector.scalar_tensor_tensor(
+                drop[t][:, half(h)], y[t, h][:], unit_sb[:, t : t + 1], lose[t][:, half(h)], ALU.mult, ALU.mult
+            )
 
         def remains(t, h):
-            cols = slice(h * HALF, (h + 1) * HALF)
-            u = unit_sb[:, t : t + 1]
-            nc.vector.scalar_tensor_tensor(kept[h][:, t, :], y[t, h][:], u, drop[t][:, cols], ALU.mult, ALU.subtract)
+            nc.vector.scalar_tensor_tensor(
+                kept[h][:, t, :], y[t, h][:], unit_sb[:, t : t + 1], drop[t][:, half(h)], ALU.mult, ALU.subtract
+            )
 
-        def fetch(t):
-            for c in range(S // CHUNK):
-                nc.scalar.activation(
-                    fetched[c][:, t, :], drop[t][:].indirect(entries(pt_sb, c * CHUNK, CHUNK)), ACT.Copy, scale=0.5
-                )
+        def fetch(t, c):
+            nc.scalar.activation(
+                fetched[c][:, t, :], drop[t][:].indirect(entries(pt_sb, c * CHUNK, CHUNK)), ACT.Copy, scale=0.5
+            )
 
-        units = [(t, h) for t in range(PACK) for h in range(HALVES)]
-        salience(*units[0])
-        for n, (t, h) in enumerate(units):
-            if n + 1 < len(units):
-                salience(*units[n + 1])
-            dropped(t, h)
-            if h == HALVES - 1:
-                fetch(t)
-                for g in range(HALVES):
-                    remains(t, g)
+        chunks = range(S // CHUNK)
+        for t in range(PACK):
+            magnitude(t)
+        salience(0, half(0))
+        salience(0, half(1))
+        for t in range(PACK + 1):
+            if t < PACK:
+                max_pairs(t)
+            if t >= 1:
+                dropped(t - 1, 0)
+            if t + 1 < PACK:
+                salience(t + 1, slice(0, S))
+            if t < PACK:
+                max_groups(t)
+            if t >= 1:
+                dropped(t - 1, 1)
+                for c in chunks:
+                    fetch(t - 1, c)
+            if t < PACK:
+                gate(t)
+        for t in range(PACK):
+            for h in range(HALVES):
+                remains(t, h)
 
         w2_bf = keep.tile([P, N * PACK], BF16, name="w2_bf", align_bytes=64)
         w2_codes = keep.tile([P, N], U32, name="w2_codes", align_bytes=64)
         w2_scales = keep.tile([P, N], U8, name="w2_scales", align_bytes=64)
         nc.scalar.copy(
-            w2_bf[:].rearrange("p (c i j) -> p c j i", i=4, j=PACK),
-            w2_raw.rearrange("p (j c i) -> p c j i", j=PACK, i=4),
+            w2_bf[:].rearrange("p (c e j) -> p c j e", e=2, j=PACK),
+            w2_raw.rearrange("p (j c e) -> p c j e", j=PACK, e=2),
         )
         nc.vector.quantize_mx(out=w2_codes[:].bitcast(FP8X4), scales=w2_scales[:], in_=w2_bf[:])
 
-        for c in range(S // CHUNK):
+        hid = {}
+
+        def hidden(c):
             h, first = divmod(c * CHUNK, HALF)
-            hid = ring.tile([P, CHUNK * PACK], BF16, name="hid", align_bytes=64)
+            hid[c] = ring.tile([P, CHUNK * PACK], BF16, name="hid", align_bytes=64)
             nc.vector.tensor_tensor(
-                hid[:].rearrange("p (c i t) -> p c t i", i=4, t=PACK),
-                kept[h][:, :, first : first + CHUNK].rearrange("p t (c i) -> p c t i", i=4),
-                fetched[c][:].rearrange("p t (c i) -> p c t i", i=4),
+                hid[c][:].rearrange("p (c e t) -> p c t e", e=2, t=PACK),
+                kept[h][:, :, first : first + CHUNK].rearrange("p t (c e) -> p c t e", e=2),
+                fetched[c][:].rearrange("p t (c e) -> p c t e", e=2),
                 ALU.add,
             )
+
+        def product(c):
             hid_codes = ring.tile([P, CHUNK], U32, name="hid_codes", align_bytes=64)
             hid_scales = ring.tile([P, CHUNK], U8, name="hid_scales", align_bytes=64)
-            nc.vector.quantize_mx(out=hid_codes[:].bitcast(FP8X4), scales=hid_scales[:], in_=hid[:])
+            nc.vector.quantize_mx(out=hid_codes[:].bitcast(FP8X4), scales=hid_scales[:], in_=hid[c][:])
             acc = psum.tile([P, CHUNK], F32, name="acc", tag="bank")
             nc.tensor.matmul_mx(
                 out=acc[:],
@@ -210,3 +229,9 @@ def tile_picked_ylisax_comp_p_kernel(
             result = ring.tile([P, CHUNK], F32, name="result")
             nc.scalar.copy(result[:], acc[:])
             nc.sync.dma_start(out[:, c * CHUNK : (c + 1) * CHUNK], result[:])
+
+        hidden(0)
+        for c in chunks:
+            if c + 1 < len(chunks):
+                hidden(c + 1)
+            product(c)

@@ -30,7 +30,7 @@ def tile_picked_ylisax_comp_p_kernel(
     nc = tc.nc
     with ExitStack() as ctx:
         keep = ctx.enter_context(tc.tile_pool(name="keep", bufs=1))
-        ring = ctx.enter_context(tc.tile_pool(name="ring", bufs=3))
+        ring = ctx.enter_context(tc.tile_pool(name="ring", bufs=4))
         psum = ctx.enter_context(tc.psum_pool(name="psum", bufs=8))
 
         offs_sb = keep.tile([P, S // STRIPE], U16, name="offs_sb")
@@ -38,13 +38,12 @@ def tile_picked_ylisax_comp_p_kernel(
         nc.sync.dma_start(offs_sb[:], offs)
 
         x_scale_win = keep.tile([P, T], U8, name="x_scale_win", align_bytes=64)
+        x_scale_rows = keep.tile([P, T], U8, name="x_scale_rows", align_bytes=64)
         nc.vector.memset(x_scale_win[:].bitcast(I32), 0)
         for q in range(4):
-            nc.gpsimd.dma_start(
-                x_scale_win[32 * q : 32 * q + 4 * PASSES, :].bitcast(I32),
-                x_scales[:, 4 * q : 4 * q + 4, :].bitcast(I32),
-            )
-
+            rows = slice(32 * q, 32 * q + 4 * PASSES)
+            nc.sync.dma_start(x_scale_rows[rows, :].bitcast(I32), x_scales[:, 4 * q : 4 * q + 4, :].bitcast(I32))
+            nc.vector.tensor_copy(x_scale_win[rows, :].bitcast(I32), x_scale_rows[rows, :].bitcast(I32))
         w1_rows = w1.rearrange("(o p j) c -> o p (j c)", p=P, j=PACK)
         w1_raw, x_win = [], []
         for o in range(PASSES):
@@ -65,12 +64,12 @@ def tile_picked_ylisax_comp_p_kernel(
             grouped = keep.tile([P, PACK * H], BF16, name=f"w1_bf{o}", align_bytes=64)
             codes = keep.tile([P, H], U32, name=f"w1_codes{o}", align_bytes=64)
             scales = keep.tile([P, H], U8, name=f"w1_scales{o}", align_bytes=64)
-            nc.scalar.activation(
-                grouped[:].rearrange("p (t m j) -> p t m j", t=PACK, j=PACK),
-                w1_raw[o][:].rearrange("p (j m t) -> p t m j", j=PACK, t=PACK),
-                ACT.Copy,
-            )
+            dealt = grouped[:].rearrange("p (t m j) -> p t m j", t=PACK, j=PACK)
+            rows = w1_raw[o][:].rearrange("p (j m t) -> p t m j", j=PACK, t=PACK)
+            if o == 1:
+                nc.vector.tensor_copy(dealt, rows)
             if o == 0:
+                nc.scalar.activation(dealt, rows, ACT.Copy)
                 for h in range(HALVES):
                     g = keep.tile([P, HALF], U8, name=f"xg_scales{h}", align_bytes=64)
                     nc.vector.tensor_copy(g[:], x_scale_win[:].indirect(entries(offs_sb, h * HALF, HALF)))
@@ -78,6 +77,7 @@ def tile_picked_ylisax_comp_p_kernel(
             nc.vector.quantize_mx(out=codes[:].bitcast(FP8X4), scales=scales[:], in_=grouped[:])
             w1_codes.append(codes)
             w1_scales.append(scales)
+        for o in range(PASSES):
             for h in range(HALVES):
                 g = keep.tile([P, HALF], U32, name=f"xg_words{o}_{h}", align_bytes=64)
                 nc.vector.tensor_copy(g[:], x_win[o][:].indirect(entries(offs_sb, h * HALF, HALF)))
@@ -111,14 +111,15 @@ def tile_picked_ylisax_comp_p_kernel(
                     )
 
         drop = [keep.tile([P, S], F32, name=f"drop{t}") for t in range(PACK)]
-        kept = [keep.tile([P, PACK, HALF], F32, name=f"kept{h}") for h in range(HALVES)]
-        fetched = [keep.tile([P, PACK, CHUNK], F32, name=f"fetched{c}") for c in range(S // CHUNK)]
+        kept = [keep.tile([P, S], F32, name=f"kept{t}") for t in range(PACK)]
+        fetched = [keep.tile([P, S], F32, name=f"fetched{t}") for t in range(PACK)]
+        comp = [keep.tile([P, PACK, HALF], F32, name=f"comp{h}") for h in range(HALVES)]
         G = S // D
-        mag = [keep.tile([P, S], F32, name=f"mag{t}") for t in range(PACK)]
+        mag = [keep.tile([P, S], F32, name=f"mag{t}", tag=f"work{t}") for t in range(PACK)]
         sal = [keep.tile([P, S], F32, name=f"sal{t}") for t in range(PACK)]
         pair = [keep.tile([P, 2 * G], F32, name=f"pair{t}") for t in range(PACK)]
         best = [keep.tile([P, G], F32, name=f"best{t}") for t in range(PACK)]
-        arg = [keep.tile([P, S], F32, name=f"arg{t}") for t in range(PACK)]
+        arg = {}
         lose = [keep.tile([P, S], F32, name=f"lose{t}") for t in range(PACK)]
 
         def half(h):
@@ -141,6 +142,7 @@ def tile_picked_ylisax_comp_p_kernel(
             nc.vector.tensor_tensor(best[t][:], pair[t][:, 0::2], pair[t][:, 1::2], ALU.max)
 
         def gate(t):
+            arg[t] = keep.tile([P, S], F32, name=f"arg{t}", tag=f"work{t}")
             nc.vector.scalar_tensor_tensor(
                 arg[t][:].rearrange("p (v d) -> p v d", d=D),
                 best[t][:].unsqueeze(2).to_broadcast([P, G, D]),
@@ -159,12 +161,12 @@ def tile_picked_ylisax_comp_p_kernel(
 
         def remains(t, h):
             nc.vector.scalar_tensor_tensor(
-                kept[h][:, t, :], y[t, h][:], unit_sb[:, t : t + 1], drop[t][:, half(h)], ALU.mult, ALU.subtract
+                kept[t][:, half(h)], y[t, h][:], unit_sb[:, t : t + 1], drop[t][:, half(h)], ALU.mult, ALU.subtract
             )
 
         def fetch(t, c):
             nc.scalar.activation(
-                fetched[c][:, t, :], drop[t][:].indirect(entries(pt_sb, c * CHUNK, CHUNK)), ACT.Copy, scale=0.5
+                fetched[t][:, c * CHUNK : (c + 1) * CHUNK], drop[t][:].indirect(entries(pt_sb, c * CHUNK, CHUNK)), ACT.Copy, scale=0.5
             )
 
         chunks = range(S // CHUNK)
@@ -190,13 +192,16 @@ def tile_picked_ylisax_comp_p_kernel(
         for t in range(PACK):
             for h in range(HALVES):
                 remains(t, h)
+        for t in range(PACK):
+            for h in range(HALVES):
+                nc.vector.tensor_tensor(comp[h][:, t, :], kept[t][:, half(h)], fetched[t][:, half(h)], ALU.add)
 
         w2_bf = keep.tile([P, N * PACK], BF16, name="w2_bf", align_bytes=64)
         w2_codes = keep.tile([P, N], U32, name="w2_codes", align_bytes=64)
         w2_scales = keep.tile([P, N], U8, name="w2_scales", align_bytes=64)
         nc.scalar.copy(
-            w2_bf[:].rearrange("p (c e j) -> p c j e", e=2, j=PACK),
-            w2_raw.rearrange("p (j c e) -> p c j e", j=PACK, e=2),
+            w2_bf[:].rearrange("p (n j) -> p n j", j=PACK),
+            w2_raw.rearrange("p (j n) -> p n j", j=PACK),
         )
         nc.vector.quantize_mx(out=w2_codes[:].bitcast(FP8X4), scales=w2_scales[:], in_=w2_bf[:])
 
@@ -205,12 +210,12 @@ def tile_picked_ylisax_comp_p_kernel(
         def hidden(c):
             h, first = divmod(c * CHUNK, HALF)
             hid[c] = ring.tile([P, CHUNK * PACK], BF16, name="hid", align_bytes=64)
-            nc.vector.tensor_tensor(
-                hid[c][:].rearrange("p (c e t) -> p c t e", e=2, t=PACK),
-                kept[h][:, :, first : first + CHUNK].rearrange("p t (c e) -> p c t e", e=2),
-                fetched[c][:].rearrange("p t (c e) -> p c t e", e=2),
-                ALU.add,
-            )
+            grouped = hid[c][:].rearrange("p (j t) -> p j t", t=PACK)
+            rows = comp[h][:, :, first : first + CHUNK].rearrange("p t j -> p j t")
+            if c == len(chunks) - 1:
+                nc.scalar.copy(grouped, rows)
+            else:
+                nc.vector.tensor_copy(grouped, rows)
 
         def product(c):
             hid_codes = ring.tile([P, CHUNK], U32, name="hid_codes", align_bytes=64)

@@ -22,6 +22,7 @@ HALF = 512
 HALVES = S // HALF
 CHUNK = 256
 STRIPE = 16
+POOL_ADDS = 5
 
 
 def tile_picked_ylisax_comp_p_kernel(
@@ -87,11 +88,20 @@ def tile_picked_ylisax_comp_p_kernel(
         xn_rows = xn.rearrange("(p t) j -> p t j", t=PACK)
         unit_sb = late[:, PACK * S + PACK * N :]
         w2_raw = late[:, PACK * S : PACK * S + PACK * N]
+        nc.sync.dma_start(w2_raw, w2.rearrange("(p j) n -> p (j n)", j=PACK))
         for t in range(PACK):
             nc.sync.dma_start(late[:, t * S : (t + 1) * S], xn_rows[:, t, :])
             if t == 1:
                 nc.sync.dma_start(unit_sb, unit.rearrange("(p t) o -> p (t o)", t=PACK))
-        nc.sync.dma_start(w2_raw, w2.rearrange("(p j) n -> p (j n)", j=PACK))
+
+        w2_bf = keep.tile([P, N * PACK], BF16, name="w2_bf", align_bytes=64)
+        w2_codes = keep.tile([P, N], U32, name="w2_codes", align_bytes=64)
+        w2_scales = keep.tile([P, N], U8, name="w2_scales", align_bytes=64)
+        nc.vector.tensor_copy(
+            w2_bf[:].rearrange("p (n j) -> p n j", j=PACK),
+            w2_raw.rearrange("p (j n) -> p n j", j=PACK),
+        )
+        nc.vector.quantize_mx(out=w2_codes[:].bitcast(FP8X4), scales=w2_scales[:], in_=w2_bf[:])
 
         y = {}
         for t in range(PACK):
@@ -113,7 +123,7 @@ def tile_picked_ylisax_comp_p_kernel(
         drop = [keep.tile([P, S], F32, name=f"drop{t}") for t in range(PACK)]
         kept = [keep.tile([P, S], F32, name=f"kept{t}") for t in range(PACK)]
         fetched = [keep.tile([P, S], F32, name=f"fetched{t}") for t in range(PACK)]
-        comp = [keep.tile([P, PACK, HALF], F32, name=f"comp{h}") for h in range(HALVES)]
+        comp = keep.tile([P, PACK * S], F32, name="comp")
         G = S // D
         mag = [keep.tile([P, S], F32, name=f"mag{t}", tag=f"work{t}") for t in range(PACK)]
         sal = [keep.tile([P, S], F32, name=f"sal{t}") for t in range(PACK)]
@@ -172,46 +182,54 @@ def tile_picked_ylisax_comp_p_kernel(
         chunks = range(S // CHUNK)
         for t in range(PACK):
             magnitude(t)
-        salience(0, half(0))
-        salience(0, half(1))
-        for t in range(PACK + 1):
-            if t < PACK:
-                max_pairs(t)
-            if t >= 1:
-                dropped(t - 1, 0)
-            if t + 1 < PACK:
-                salience(t + 1, slice(0, S))
-            if t < PACK:
-                max_groups(t)
-            if t >= 1:
-                dropped(t - 1, 1)
-                for c in chunks:
-                    fetch(t - 1, c)
-            if t < PACK:
-                gate(t)
-        for t in range(PACK):
+        by_chunk = comp[:].rearrange("p (c t j) -> p c t j", t=PACK, j=CHUNK)
+
+        def compensate(engine, t, first, count):
+            cols = slice(first * CHUNK, (first + count) * CHUNK)
+            engine.tensor_tensor(
+                by_chunk[:, first : first + count, t, :],
+                kept[t][:, cols].rearrange("p (c j) -> p c j", j=CHUNK),
+                fetched[t][:, cols].rearrange("p (c j) -> p c j", j=CHUNK),
+                ALU.add,
+            )
+
+        def front(tiles):
+            for t in tiles:
+                for h in range(HALVES):
+                    salience(t, half(h))
+            for step in (max_pairs, max_groups, gate):
+                for t in tiles:
+                    step(t)
+
+        def drop_and_fetch(t):
+            for h in range(HALVES):
+                dropped(t, h)
+            for c in chunks:
+                fetch(t, c)
+
+        def keep_part(t):
             for h in range(HALVES):
                 remains(t, h)
-        for t in range(PACK):
-            for h in range(HALVES):
-                nc.vector.tensor_tensor(comp[h][:, t, :], kept[t][:, half(h)], fetched[t][:, half(h)], ALU.add)
+                if t * HALVES + h < POOL_ADDS:
+                    compensate(nc.gpsimd, t, h * (HALF // CHUNK), HALF // CHUNK)
 
-        w2_bf = keep.tile([P, N * PACK], BF16, name="w2_bf", align_bytes=64)
-        w2_codes = keep.tile([P, N], U32, name="w2_codes", align_bytes=64)
-        w2_scales = keep.tile([P, N], U8, name="w2_scales", align_bytes=64)
-        nc.scalar.copy(
-            w2_bf[:].rearrange("p (n j) -> p n j", j=PACK),
-            w2_raw.rearrange("p (j n) -> p n j", j=PACK),
-        )
-        nc.vector.quantize_mx(out=w2_codes[:].bitcast(FP8X4), scales=w2_scales[:], in_=w2_bf[:])
+        front((0, 1))
+        drop_and_fetch(0)
+        drop_and_fetch(1)
+        front((2, 3))
+        for t in (2, 3):
+            keep_part(t - 2)
+            drop_and_fetch(t)
+        for t in (2, 3):
+            keep_part(t)
+        compensate(nc.vector, 2, HALF // CHUNK, HALF // CHUNK)
 
         hid = {}
 
         def hidden(c):
-            h, first = divmod(c * CHUNK, HALF)
             hid[c] = ring.tile([P, CHUNK * PACK], BF16, name="hid", align_bytes=64)
             grouped = hid[c][:].rearrange("p (j t) -> p j t", t=PACK)
-            rows = comp[h][:, :, first : first + CHUNK].rearrange("p t j -> p j t")
+            rows = comp[:, c * PACK * CHUNK : (c + 1) * PACK * CHUNK].rearrange("p (t j) -> p j t", t=PACK)
             if c == len(chunks) - 1:
                 nc.scalar.copy(grouped, rows)
             else:
@@ -235,8 +253,10 @@ def tile_picked_ylisax_comp_p_kernel(
             nc.scalar.copy(result[:], acc[:])
             nc.sync.dma_start(out[:, c * CHUNK : (c + 1) * CHUNK], result[:])
 
-        hidden(0)
-        for c in chunks:
-            if c + 1 < len(chunks):
-                hidden(c + 1)
-            product(c)
+        for step in range(len(chunks) + 2):
+            if step < len(chunks):
+                compensate(nc.vector, PACK - 1, step, 1)
+            if 1 <= step <= len(chunks):
+                hidden(step - 1)
+            if step >= 2:
+                product(step - 2)

@@ -17,11 +17,17 @@ ACT = mybir.ActivationFunctionType
 
 P = 128
 PACK = 4
+LAST = PACK - 1
 PASSES = K // (P * PACK)
+QUADRANT = 32
+SCALE_ROWS = 4
+STRIPE = 16
 HALF = 512
 HALVES = S // HALF
 CHUNK = 256
-STRIPE = 16
+CHUNKS = S // CHUNK
+PER_HALF = HALF // CHUNK
+GROUPS = S // D
 POOL_ADDS = 5
 
 
@@ -31,8 +37,14 @@ def tile_picked_ylisax_comp_p_kernel(
     nc = tc.nc
     with ExitStack() as ctx:
         keep = ctx.enter_context(tc.tile_pool(name="keep", bufs=1))
-        ring = ctx.enter_context(tc.tile_pool(name="ring", bufs=4))
-        psum = ctx.enter_context(tc.psum_pool(name="psum", bufs=8))
+        ring = ctx.enter_context(tc.tile_pool(name="ring", bufs=CHUNKS))
+        psum = ctx.enter_context(tc.psum_pool(name="psum", bufs=PACK * HALVES))
+
+        def entries(list_sb, first, count):
+            return list_sb[:, first // STRIPE : (first + count) // STRIPE]
+
+        def half(h):
+            return slice(h * HALF, (h + 1) * HALF)
 
         offs_sb = keep.tile([P, S // STRIPE], U16, name="offs_sb")
         pt_sb = keep.tile([P, S // STRIPE], U16, name="pt_sb")
@@ -41,10 +53,12 @@ def tile_picked_ylisax_comp_p_kernel(
         x_scale_win = keep.tile([P, T], U8, name="x_scale_win", align_bytes=64)
         x_scale_rows = keep.tile([P, T], U8, name="x_scale_rows", align_bytes=64)
         nc.vector.memset(x_scale_win[:].bitcast(I32), 0)
-        for q in range(4):
-            rows = slice(32 * q, 32 * q + 4 * PASSES)
-            nc.sync.dma_start(x_scale_rows[rows, :].bitcast(I32), x_scales[:, 4 * q : 4 * q + 4, :].bitcast(I32))
-            nc.vector.tensor_copy(x_scale_win[rows, :].bitcast(I32), x_scale_rows[rows, :].bitcast(I32))
+        for q in range(P // QUADRANT):
+            live = slice(QUADRANT * q, QUADRANT * q + SCALE_ROWS * PASSES)
+            source = x_scales[:, SCALE_ROWS * q : SCALE_ROWS * (q + 1), :]
+            nc.sync.dma_start(x_scale_rows[live, :].bitcast(I32), source.bitcast(I32))
+            nc.vector.tensor_copy(x_scale_win[live, :].bitcast(I32), x_scale_rows[live, :].bitcast(I32))
+
         w1_rows = w1.rearrange("(o p j) c -> o p (j c)", p=P, j=PACK)
         w1_raw, x_win = [], []
         for o in range(PASSES):
@@ -57,40 +71,36 @@ def tile_picked_ylisax_comp_p_kernel(
             x_win.append(win)
         nc.sync.dma_start(pt_sb[:], pt)
 
-        def entries(lst, first, count):
-            return lst[:, first // STRIPE : (first + count) // STRIPE]
-
         w1_codes, w1_scales, xg_scales, xg_words = [], [], [], {}
         for o in range(PASSES):
-            grouped = keep.tile([P, PACK * H], BF16, name=f"w1_bf{o}", align_bytes=64)
+            w1_bf = keep.tile([P, PACK * H], BF16, name=f"w1_bf{o}", align_bytes=64)
             codes = keep.tile([P, H], U32, name=f"w1_codes{o}", align_bytes=64)
             scales = keep.tile([P, H], U8, name=f"w1_scales{o}", align_bytes=64)
-            dealt = grouped[:].rearrange("p (t m j) -> p t m j", t=PACK, j=PACK)
-            rows = w1_raw[o][:].rearrange("p (j m t) -> p t m j", j=PACK, t=PACK)
-            if o == 1:
-                nc.vector.tensor_copy(dealt, rows)
+            dealt = w1_bf[:].rearrange("p (t m j) -> p t m j", t=PACK, j=PACK)
+            given = w1_raw[o][:].rearrange("p (j m t) -> p t m j", j=PACK, t=PACK)
+            nc.scalar.activation(dealt[:, : PACK // 2], given[:, : PACK // 2], ACT.Copy)
+            nc.vector.tensor_copy(dealt[:, PACK // 2 :], given[:, PACK // 2 :])
             if o == 0:
-                nc.scalar.activation(dealt, rows, ACT.Copy)
                 for h in range(HALVES):
-                    g = keep.tile([P, HALF], U8, name=f"xg_scales{h}", align_bytes=64)
-                    nc.vector.tensor_copy(g[:], x_scale_win[:].indirect(entries(offs_sb, h * HALF, HALF)))
-                    xg_scales.append(g)
-            nc.vector.quantize_mx(out=codes[:].bitcast(FP8X4), scales=scales[:], in_=grouped[:])
+                    picked = keep.tile([P, HALF], U8, name=f"xg_scales{h}", align_bytes=64)
+                    nc.vector.tensor_copy(picked[:], x_scale_win[:].indirect(entries(offs_sb, h * HALF, HALF)))
+                    xg_scales.append(picked)
+            nc.vector.quantize_mx(out=codes[:].bitcast(FP8X4), scales=scales[:], in_=w1_bf[:])
             w1_codes.append(codes)
             w1_scales.append(scales)
         for o in range(PASSES):
             for h in range(HALVES):
-                g = keep.tile([P, HALF], U32, name=f"xg_words{o}_{h}", align_bytes=64)
-                nc.vector.tensor_copy(g[:], x_win[o][:].indirect(entries(offs_sb, h * HALF, HALF)))
-                xg_words[o, h] = g
+                xg_words[o, h] = keep.tile([P, HALF], U32, name=f"xg_words{o}_{h}", align_bytes=64)
+                nc.vector.tensor_copy(xg_words[o, h][:], x_win[o][:].indirect(entries(offs_sb, h * HALF, HALF)))
 
         late = keep.tile([P, PACK * S + PACK * N + PACK], F32, name="late", tag="stage0")
-        xn_rows = xn.rearrange("(p t) j -> p t j", t=PACK)
-        unit_sb = late[:, PACK * S + PACK * N :]
+        xn_sb = [late[:, t * S : (t + 1) * S] for t in range(PACK)]
         w2_raw = late[:, PACK * S : PACK * S + PACK * N]
+        unit_sb = late[:, PACK * S + PACK * N :]
+        xn_rows = xn.rearrange("(p t) j -> p t j", t=PACK)
         nc.sync.dma_start(w2_raw, w2.rearrange("(p j) n -> p (j n)", j=PACK))
         for t in range(PACK):
-            nc.sync.dma_start(late[:, t * S : (t + 1) * S], xn_rows[:, t, :])
+            nc.sync.dma_start(xn_sb[t], xn_rows[:, t, :])
             if t == 1:
                 nc.sync.dma_start(unit_sb, unit.rearrange("(p t) o -> p (t o)", t=PACK))
 
@@ -115,130 +125,118 @@ def tile_picked_ylisax_comp_p_kernel(
                         lhsT=w1_codes[o][:, t * P : (t + 1) * P].bitcast(FP8X4),
                         lhsT_scale=w1_scales[o][:, t * P : (t + 1) * P],
                         rhs=xg_words[o, h][:].bitcast(FP8X4),
-                        rhs_scale=xg_scales[h][4 * o : P, :],
+                        rhs_scale=xg_scales[h][SCALE_ROWS * o : P, :],
                         start=(o == 0),
                         stop=(o == PASSES - 1),
                     )
 
-        drop = [keep.tile([P, S], F32, name=f"drop{t}") for t in range(PACK)]
+        wide = keep.tile([P, 2 * S], F32, name="wide")
+        drop = [keep.tile([P, S], F32, name=f"drop{t}")[:] for t in range(LAST)] + [wide[:, 0:S]]
+        window = drop[:LAST] + [wide[:]]
         kept = [keep.tile([P, S], F32, name=f"kept{t}") for t in range(PACK)]
         fetched = [keep.tile([P, S], F32, name=f"fetched{t}") for t in range(PACK)]
-        comp = keep.tile([P, PACK * S], F32, name="comp")
-        G = S // D
+        hid = keep.tile([P, PACK * S], F32, name="hid")
+        hid_by_chunk = hid[:].rearrange("p (c t j) -> p c t j", t=PACK, j=CHUNK)
         mag = [keep.tile([P, S], F32, name=f"mag{t}", tag=f"work{t}") for t in range(PACK)]
-        sal = [keep.tile([P, S], F32, name=f"sal{t}") for t in range(PACK)]
-        pair = [keep.tile([P, 2 * G], F32, name=f"pair{t}") for t in range(PACK)]
-        best = [keep.tile([P, G], F32, name=f"best{t}") for t in range(PACK)]
-        arg = {}
-        lose = [keep.tile([P, S], F32, name=f"lose{t}") for t in range(PACK)]
+        pair = [keep.tile([P, 2 * GROUPS], F32, name=f"pair{t}") for t in range(PACK)]
+        best = [keep.tile([P, GROUPS], F32, name=f"best{t}") for t in range(PACK)]
+        lose = [keep.tile([P, S], F32, name=f"lose{t}")[:] for t in range(LAST)] + [wide[:, S : 2 * S]]
+        sal = {}
 
-        def half(h):
-            return slice(h * HALF, (h + 1) * HALF)
-
-        def magnitude(t):
+        def salience(t):
+            engine, tag = (nc.gpsimd, "sal1") if t == LAST else (nc.vector, f"sal{t}")
+            sal[t] = keep.tile([P, S], F32, name=f"sal{t}", tag=tag)
             for h in range(HALVES):
-                nc.scalar.activation(mag[t][:, half(h)], y[t, h][:], ACT.Abs)
-
-        def salience(t, cols):
-            nc.vector.tensor_tensor(sal[t][:, cols], mag[t][:, cols], late[:, t * S : (t + 1) * S][:, cols], ALU.mult)
+                engine.tensor_tensor(sal[t][:, half(h)], mag[t][:, half(h)], xn_sb[t][:, half(h)], ALU.mult)
 
         def max_pairs(t):
-            groups = sal[t][:].rearrange("p (v d) -> p v d", d=D)
+            members = sal[t][:].rearrange("p (v d) -> p v d", d=D)
             nc.vector.tensor_tensor(
-                pair[t][:].rearrange("p (v e) -> p v e", e=2), groups[:, :, 0:2], groups[:, :, 2:4], ALU.max
+                pair[t][:].rearrange("p (v e) -> p v e", e=2), members[:, :, 0:2], members[:, :, 2:4], ALU.max
             )
 
         def max_groups(t):
             nc.vector.tensor_tensor(best[t][:], pair[t][:, 0::2], pair[t][:, 1::2], ALU.max)
 
         def gate(t):
-            arg[t] = keep.tile([P, S], F32, name=f"arg{t}", tag=f"work{t}")
+            margin = keep.tile([P, S], F32, name=f"margin{t}", tag=f"work{t}")
             nc.vector.scalar_tensor_tensor(
-                arg[t][:].rearrange("p (v d) -> p v d", d=D),
-                best[t][:].unsqueeze(2).to_broadcast([P, G, D]),
+                margin[:].rearrange("p (v d) -> p v d", d=D),
+                best[t][:].unsqueeze(2).to_broadcast([P, GROUPS, D]),
                 -0.6,
                 sal[t][:].rearrange("p (v d) -> p v d", d=D),
                 ALU.mult,
                 ALU.add,
             )
             for h in range(HALVES):
-                nc.scalar.activation(lose[t][:, half(h)], arg[t][:, half(h)], ACT.Sigmoid, scale=-5.0)
+                nc.scalar.activation(lose[t][:, half(h)], margin[:, half(h)], ACT.Sigmoid, scale=-5.0)
 
-        def dropped(t, h):
-            nc.vector.scalar_tensor_tensor(
-                drop[t][:, half(h)], y[t, h][:], unit_sb[:, t : t + 1], lose[t][:, half(h)], ALU.mult, ALU.mult
-            )
-
-        def remains(t, h):
-            nc.vector.scalar_tensor_tensor(
-                kept[t][:, half(h)], y[t, h][:], unit_sb[:, t : t + 1], drop[t][:, half(h)], ALU.mult, ALU.subtract
-            )
-
-        def fetch(t, c):
-            nc.scalar.activation(
-                fetched[t][:, c * CHUNK : (c + 1) * CHUNK], drop[t][:].indirect(entries(pt_sb, c * CHUNK, CHUNK)), ACT.Copy, scale=0.5
-            )
-
-        chunks = range(S // CHUNK)
-        for t in range(PACK):
-            magnitude(t)
-        by_chunk = comp[:].rearrange("p (c t j) -> p c t j", t=PACK, j=CHUNK)
-
-        def compensate(engine, t, first, count):
-            cols = slice(first * CHUNK, (first + count) * CHUNK)
-            engine.tensor_tensor(
-                by_chunk[:, first : first + count, t, :],
-                kept[t][:, cols].rearrange("p (c j) -> p c j", j=CHUNK),
-                fetched[t][:, cols].rearrange("p (c j) -> p c j", j=CHUNK),
-                ALU.add,
-            )
-
-        def front(tiles):
-            for t in tiles:
-                for h in range(HALVES):
-                    salience(t, half(h))
-            for step in (max_pairs, max_groups, gate):
-                for t in tiles:
+        def gates(slots):
+            for step in (salience, max_pairs, max_groups, gate):
+                for t in slots:
                     step(t)
 
         def drop_and_fetch(t):
             for h in range(HALVES):
-                dropped(t, h)
-            for c in chunks:
-                fetch(t, c)
+                nc.vector.scalar_tensor_tensor(
+                    drop[t][:, half(h)], y[t, h][:], unit_sb[:, t : t + 1], lose[t][:, half(h)], ALU.mult, ALU.mult
+                )
+            for c in range(PER_HALF if t == LAST else CHUNKS):
+                nc.scalar.activation(
+                    fetched[t][:, c * CHUNK : (c + 1) * CHUNK],
+                    window[t].indirect(entries(pt_sb, c * CHUNK, CHUNK)),
+                    ACT.Copy,
+                    scale=0.5,
+                )
+
+        def compensate(engine, t, h):
+            engine.tensor_tensor(
+                hid_by_chunk[:, h * PER_HALF : (h + 1) * PER_HALF, t, :],
+                kept[t][:, half(h)].rearrange("p (c j) -> p c j", j=CHUNK),
+                fetched[t][:, half(h)].rearrange("p (c j) -> p c j", j=CHUNK),
+                ALU.add,
+            )
 
         def keep_part(t):
             for h in range(HALVES):
-                remains(t, h)
+                nc.vector.scalar_tensor_tensor(
+                    kept[t][:, half(h)], y[t, h][:], unit_sb[:, t : t + 1], drop[t][:, half(h)], ALU.mult, ALU.subtract
+                )
                 if t * HALVES + h < POOL_ADDS:
-                    compensate(nc.gpsimd, t, h * (HALF // CHUNK), HALF // CHUNK)
+                    compensate(nc.gpsimd, t, h)
 
-        front((0, 1))
-        drop_and_fetch(0)
-        drop_and_fetch(1)
-        front((2, 3))
-        for t in (2, 3):
-            keep_part(t - 2)
+        for t in range(PACK):
+            for h in range(HALVES):
+                nc.scalar.activation(mag[t][:, half(h)], y[t, h][:], ACT.Abs)
+        early, later = range(0, PACK // 2), range(PACK // 2, PACK)
+        gates(early)
+        for t in early:
             drop_and_fetch(t)
-        for t in (2, 3):
-            keep_part(t)
-        compensate(nc.vector, 2, HALF // CHUNK, HALF // CHUNK)
+        gates(later)
+        for step, slots in ((keep_part, early), (drop_and_fetch, later), (keep_part, later)):
+            for t in slots:
+                step(t)
+        nc.vector.tensor_scalar(
+            fetched[LAST][:, half(1)], window[LAST].indirect(entries(pt_sb, HALF, HALF)), 0.5, 0.0, ALU.mult, ALU.add
+        )
+        for t, h in [divmod(n, HALVES) for n in range(POOL_ADDS, LAST * HALVES)]:
+            compensate(nc.vector, t, h)
 
-        hid = {}
-
-        def hidden(c):
-            hid[c] = ring.tile([P, CHUNK * PACK], BF16, name="hid", align_bytes=64)
-            grouped = hid[c][:].rearrange("p (j t) -> p j t", t=PACK)
-            rows = comp[:, c * PACK * CHUNK : (c + 1) * PACK * CHUNK].rearrange("p (t j) -> p j t", t=PACK)
-            if c == len(chunks) - 1:
-                nc.scalar.copy(grouped, rows)
-            else:
-                nc.vector.tensor_copy(grouped, rows)
-
-        def product(c):
+        halves = list(reversed(range(HALVES)))
+        for h in halves:
+            compensate(nc.vector, LAST, h)
+        hid_bf = {}
+        for h in halves:
+            for c, copy in ((h * PER_HALF, nc.scalar.copy), (h * PER_HALF + 1, nc.vector.tensor_copy)):
+                hid_bf[c] = ring.tile([P, CHUNK * PACK], BF16, name="hid_bf", align_bytes=64)
+                copy(
+                    hid_bf[c][:].rearrange("p (j t) -> p j t", t=PACK),
+                    hid[:, c * PACK * CHUNK : (c + 1) * PACK * CHUNK].rearrange("p (t j) -> p j t", t=PACK),
+                )
+        for c in reversed(range(CHUNKS)):
             hid_codes = ring.tile([P, CHUNK], U32, name="hid_codes", align_bytes=64)
             hid_scales = ring.tile([P, CHUNK], U8, name="hid_scales", align_bytes=64)
-            nc.vector.quantize_mx(out=hid_codes[:].bitcast(FP8X4), scales=hid_scales[:], in_=hid[c][:])
+            nc.vector.quantize_mx(out=hid_codes[:].bitcast(FP8X4), scales=hid_scales[:], in_=hid_bf[c][:])
             acc = psum.tile([P, CHUNK], F32, name="acc", tag="bank")
             nc.tensor.matmul_mx(
                 out=acc[:],
@@ -252,11 +250,3 @@ def tile_picked_ylisax_comp_p_kernel(
             result = ring.tile([P, CHUNK], F32, name="result")
             nc.scalar.copy(result[:], acc[:])
             nc.sync.dma_start(out[:, c * CHUNK : (c + 1) * CHUNK], result[:])
-
-        for step in range(len(chunks) + 2):
-            if step < len(chunks):
-                compensate(nc.vector, PACK - 1, step, 1)
-            if 1 <= step <= len(chunks):
-                hidden(step - 1)
-            if step >= 2:
-                product(step - 2)

from contextlib import ExitStack

import concourse.mybir as mybir

K, T, S, D, N, H = 1024, 4096, 1024, 4, 128, 512
FLOPS = 2 * K * H * S + 2 * H * N * S

F32 = mybir.dt.float32
BF16 = mybir.dt.bfloat16
I32 = mybir.dt.int32
U32 = mybir.dt.uint32
U16 = mybir.dt.uint16
U8 = mybir.dt.uint8
FP8X4 = mybir.dt.float8_e4m3fn_x4
ALU = mybir.AluOpType
ACT = mybir.ActivationFunctionType

P = 128
PACK = 4
LAST = PACK - 1
PASSES = K // (P * PACK)
QUADRANT = 32
SCALE_ROWS = 4
STRIPE = 16
HALF = 512
HALVES = S // HALF
CHUNK = 256
CHUNKS = S // CHUNK
PER_HALF = HALF // CHUNK
GROUPS = S // D
POOL_ADDS = 5


def tile_picked_ylisax_comp_p_kernel(
    tc, x_words, x_scales, w1, xn, unit, w2, offs, pt, out
):
    nc = tc.nc
    with ExitStack() as ctx:
        keep = ctx.enter_context(tc.tile_pool(name="keep", bufs=1))
        ring = ctx.enter_context(tc.tile_pool(name="ring", bufs=CHUNKS))
        psum = ctx.enter_context(tc.psum_pool(name="psum", bufs=PACK * HALVES))

        def entries(list_sb, first, count):
            return list_sb[:, first // STRIPE : (first + count) // STRIPE]

        def half(h):
            return slice(h * HALF, (h + 1) * HALF)

        offs_sb = keep.tile([P, S // STRIPE], U16, name="offs_sb")
        pt_sb = keep.tile([P, S // STRIPE], U16, name="pt_sb")
        nc.sync.dma_start(offs_sb[:], offs)

        x_scale_win = keep.tile([P, T], U8, name="x_scale_win", align_bytes=64)
        x_scale_rows = keep.tile([P, T], U8, name="x_scale_rows", align_bytes=64)
        nc.vector.memset(x_scale_win[:].bitcast(I32), 0)
        for q in range(P // QUADRANT):
            live = slice(QUADRANT * q, QUADRANT * q + SCALE_ROWS * PASSES)
            source = x_scales[:, SCALE_ROWS * q : SCALE_ROWS * (q + 1), :]
            nc.sync.dma_start(x_scale_rows[live, :].bitcast(I32), source.bitcast(I32))
            nc.vector.tensor_copy(x_scale_win[live, :].bitcast(I32), x_scale_rows[live, :].bitcast(I32))

        w1_rows = w1.rearrange("(o p j) c -> o p (j c)", p=P, j=PACK)
        w1_raw, x_win = [], []
        for o in range(PASSES):
            raw = keep.tile([P, PACK * H], F32, name=f"w1_raw{o}", tag=f"stage{o}")
            nc.sync.dma_start(raw[:], w1_rows[o])
            w1_raw.append(raw)
        for o in range(PASSES):
            win = keep.tile([P, T], U32, name=f"x_win{o}", align_bytes=64)
            nc.sync.dma_start(win[:].bitcast(I32), x_words[o].rearrange("p n t -> p (n t)").bitcast(I32))
            x_win.append(win)
        nc.sync.dma_start(pt_sb[:], pt)

        w1_codes, w1_scales, xg_scales, xg_words = [], [], [], {}
        for o in range(PASSES):
            w1_bf = keep.tile([P, PACK * H], BF16, name=f"w1_bf{o}", align_bytes=64)
            codes = keep.tile([P, H], U32, name=f"w1_codes{o}", align_bytes=64)
            scales = keep.tile([P, H], U8, name=f"w1_scales{o}", align_bytes=64)
            dealt = w1_bf[:].rearrange("p (t m j) -> p t m j", t=PACK, j=PACK)
            given = w1_raw[o][:].rearrange("p (j m t) -> p t m j", j=PACK, t=PACK)
            nc.scalar.activation(dealt[:, : PACK // 2], given[:, : PACK // 2], ACT.Copy)
            nc.vector.tensor_copy(dealt[:, PACK // 2 :], given[:, PACK // 2 :])
            if o == 0:
                for h in range(HALVES):
                    picked = keep.tile([P, HALF], U8, name=f"xg_scales{h}", align_bytes=64)
                    nc.vector.tensor_copy(picked[:], x_scale_win[:].indirect(entries(offs_sb, h * HALF, HALF)))
                    xg_scales.append(picked)
            nc.vector.quantize_mx(out=codes[:].bitcast(FP8X4), scales=scales[:], in_=w1_bf[:])
            w1_codes.append(codes)
            w1_scales.append(scales)
        for o in range(PASSES):
            for h in range(HALVES):
                xg_words[o, h] = keep.tile([P, HALF], U32, name=f"xg_words{o}_{h}", align_bytes=64)
                nc.vector.tensor_copy(xg_words[o, h][:], x_win[o][:].indirect(entries(offs_sb, h * HALF, HALF)))

        late = keep.tile([P, PACK * S + PACK * N + PACK], F32, name="late", tag="stage0")
        xn_sb = [late[:, t * S : (t + 1) * S] for t in range(PACK)]
        w2_raw = late[:, PACK * S : PACK * S + PACK * N]
        unit_sb = late[:, PACK * S + PACK * N :]
        xn_rows = xn.rearrange("(p t) j -> p t j", t=PACK)
        nc.sync.dma_start(w2_raw, w2.rearrange("(p j) n -> p (j n)", j=PACK))
        for t in range(PACK):
            nc.sync.dma_start(xn_sb[t], xn_rows[:, t, :])
            if t == 1:
                nc.sync.dma_start(unit_sb, unit.rearrange("(p t) o -> p (t o)", t=PACK))

        w2_bf = keep.tile([P, N * PACK], BF16, name="w2_bf", align_bytes=64)
        w2_codes = keep.tile([P, N], U32, name="w2_codes", align_bytes=64)
        w2_scales = keep.tile([P, N], U8, name="w2_scales", align_bytes=64)
        nc.vector.tensor_copy(
            w2_bf[:].rearrange("p (n j) -> p n j", j=PACK),
            w2_raw.rearrange("p (j n) -> p n j", j=PACK),
        )
        nc.vector.quantize_mx(out=w2_codes[:].bitcast(FP8X4), scales=w2_scales[:], in_=w2_bf[:])

        y = {}
        for t in range(PACK):
            for h in range(HALVES):
                y[t, h] = psum.tile([P, HALF], F32, name=f"y{t}_{h}", tag="bank")
        for o in range(PASSES):
            for t in range(PACK):
                for h in range(HALVES):
                    nc.tensor.matmul_mx(
                        out=y[t, h][:],
                        lhsT=w1_codes[o][:, t * P : (t + 1) * P].bitcast(FP8X4),
                        lhsT_scale=w1_scales[o][:, t * P : (t + 1) * P],
                        rhs=xg_words[o, h][:].bitcast(FP8X4),
                        rhs_scale=xg_scales[h][SCALE_ROWS * o : P, :],
                        start=(o == 0),
                        stop=(o == PASSES - 1),
                    )

        wide = keep.tile([P, 2 * S], F32, name="wide")
        drop = [keep.tile([P, S], F32, name=f"drop{t}")[:] for t in range(LAST)] + [wide[:, 0:S]]
        window = drop[:LAST] + [wide[:]]
        kept = [keep.tile([P, S], F32, name=f"kept{t}") for t in range(PACK)]
        fetched = [keep.tile([P, S], F32, name=f"fetched{t}") for t in range(PACK)]
        hid = keep.tile([P, PACK * S], F32, name="hid")
        hid_by_chunk = hid[:].rearrange("p (c t j) -> p c t j", t=PACK, j=CHUNK)
        mag = [keep.tile([P, S], F32, name=f"mag{t}", tag=f"work{t}") for t in range(PACK)]
        pair = [keep.tile([P, 2 * GROUPS], F32, name=f"pair{t}") for t in range(PACK)]
        best = [keep.tile([P, GROUPS], F32, name=f"best{t}") for t in range(PACK)]
        lose = [keep.tile([P, S], F32, name=f"lose{t}")[:] for t in range(LAST)] + [wide[:, S : 2 * S]]
        sal = {}

        def salience(t):
            engine, tag = (nc.gpsimd, "sal1") if t == LAST else (nc.vector, f"sal{t}")
            sal[t] = keep.tile([P, S], F32, name=f"sal{t}", tag=tag)
            for h in range(HALVES):
                engine.tensor_tensor(sal[t][:, half(h)], mag[t][:, half(h)], xn_sb[t][:, half(h)], ALU.mult)

        def max_pairs(t):
            members = sal[t][:].rearrange("p (v d) -> p v d", d=D)
            nc.vector.tensor_tensor(
                pair[t][:].rearrange("p (v e) -> p v e", e=2), members[:, :, 0:2], members[:, :, 2:4], ALU.max
            )

        def max_groups(t):
            nc.vector.tensor_tensor(best[t][:], pair[t][:, 0::2], pair[t][:, 1::2], ALU.max)

        def gate(t):
            margin = keep.tile([P, S], F32, name=f"margin{t}", tag=f"work{t}")
            nc.vector.scalar_tensor_tensor(
                margin[:].rearrange("p (v d) -> p v d", d=D),
                best[t][:].unsqueeze(2).to_broadcast([P, GROUPS, D]),
                -0.6,
                sal[t][:].rearrange("p (v d) -> p v d", d=D),
                ALU.mult,
                ALU.add,
            )
            for h in range(HALVES):
                nc.scalar.activation(lose[t][:, half(h)], margin[:, half(h)], ACT.Sigmoid, scale=-5.0)

        def gates(slots):
            for step in (salience, max_pairs, max_groups, gate):
                for t in slots:
                    step(t)

        def drop_and_fetch(t):
            for h in range(HALVES):
                nc.vector.scalar_tensor_tensor(
                    drop[t][:, half(h)], y[t, h][:], unit_sb[:, t : t + 1], lose[t][:, half(h)], ALU.mult, ALU.mult
                )
            for c in range(PER_HALF if t == LAST else CHUNKS):
                nc.scalar.activation(
                    fetched[t][:, c * CHUNK : (c + 1) * CHUNK],
                    window[t].indirect(entries(pt_sb, c * CHUNK, CHUNK)),
                    ACT.Copy,
                    scale=0.5,
                )

        def compensate(engine, t, h):
            engine.tensor_tensor(
                hid_by_chunk[:, h * PER_HALF : (h + 1) * PER_HALF, t, :],
                kept[t][:, half(h)].rearrange("p (c j) -> p c j", j=CHUNK),
                fetched[t][:, half(h)].rearrange("p (c j) -> p c j", j=CHUNK),
                ALU.add,
            )

        def keep_part(t):
            for h in range(HALVES):
                nc.vector.scalar_tensor_tensor(
                    kept[t][:, half(h)], y[t, h][:], unit_sb[:, t : t + 1], drop[t][:, half(h)], ALU.mult, ALU.subtract
                )
                if t * HALVES + h < POOL_ADDS:
                    compensate(nc.gpsimd, t, h)

        for t in range(PACK):
            for h in range(HALVES):
                nc.scalar.activation(mag[t][:, half(h)], y[t, h][:], ACT.Abs)
        early, later = range(0, PACK // 2), range(PACK // 2, PACK)
        gates(early)
        for t in early:
            drop_and_fetch(t)
        gates(later)
        for step, slots in ((keep_part, early), (drop_and_fetch, later), (keep_part, later)):
            for t in slots:
                step(t)
        nc.vector.tensor_scalar(
            fetched[LAST][:, half(1)], window[LAST].indirect(entries(pt_sb, HALF, HALF)), 0.5, 0.0, ALU.mult, ALU.add
        )
        for t, h in [divmod(n, HALVES) for n in range(POOL_ADDS, LAST * HALVES)]:
            compensate(nc.vector, t, h)

        halves = list(reversed(range(HALVES)))
        for h in halves:
            compensate(nc.vector, LAST, h)
        hid_bf = {}
        for h in halves:
            for c, copy in ((h * PER_HALF, nc.scalar.copy), (h * PER_HALF + 1, nc.vector.tensor_copy)):
                hid_bf[c] = ring.tile([P, CHUNK * PACK], BF16, name="hid_bf", align_bytes=64)
                copy(
                    hid_bf[c][:].rearrange("p (j t) -> p j t", t=PACK),
                    hid[:, c * PACK * CHUNK : (c + 1) * PACK * CHUNK].rearrange("p (t j) -> p j t", t=PACK),
                )
        for c in reversed(range(CHUNKS)):
            hid_codes = ring.tile([P, CHUNK], U32, name="hid_codes", align_bytes=64)
            hid_scales = ring.tile([P, CHUNK], U8, name="hid_scales", align_bytes=64)
            nc.vector.quantize_mx(out=hid_codes[:].bitcast(FP8X4), scales=hid_scales[:], in_=hid_bf[c][:])
            acc = psum.tile([P, CHUNK], F32, name="acc", tag="bank")
            nc.tensor.matmul_mx(
                out=acc[:],
                lhsT=w2_codes[:].bitcast(FP8X4),
                lhsT_scale=w2_scales[:],
                rhs=hid_codes[:].bitcast(FP8X4),
                rhs_scale=hid_scales[:],
                start=True,
                stop=True,
            )
            result = ring.tile([P, CHUNK], F32, name="result")
            nc.scalar.copy(result[:], acc[:])
            nc.sync.dma_start(out[:, c * CHUNK : (c + 1) * CHUNK], result[:])
